import numpy as np
import ml_dtypes


def mxq(x, axis, fmt="e4m3"):
    dtype, down = {"e4m3": (ml_dtypes.float8_e4m3fn, 7), "e5m2": (ml_dtypes.float8_e5m2, 14)}[fmt]
    v = np.moveaxis(np.asarray(x, np.float32).astype(ml_dtypes.bfloat16).astype(np.float64), axis, -1)
    blocks = v.reshape(v.shape[:-1] + (-1, 32))
    amax = np.abs(blocks).max(-1, keepdims=True)
    byte = np.maximum(np.where(amax > 0, np.frexp(amax)[1] - 1 + 127, 0) - down, 1)
    scale = np.exp2(byte - 127.0)
    codes = (blocks / scale).astype(np.float32).astype(dtype).astype(np.float64)
    return np.moveaxis((codes * scale).reshape(v.shape), -1, axis)


WIDE = False


def mx_kscale(k):
    if not WIDE:
        return np.ones(k)
    levels = np.array([10, -10, 5, -5, 0])
    if k % 512:
        return np.exp2(np.random.permutation(np.resize(levels, k // 32))).repeat(32)
    a = np.empty((k // 512, 16))
    for p in range(k // 512):
        a[p, :8] = np.random.permutation(np.resize(levels, 8))
        for g in range(8):
            far = levels[np.abs(levels - a[p, g]) >= 10]
            a[p, g + 8] = far[np.random.randint(len(far))]
    return np.exp2(a.ravel()).repeat(32)


def f64(x):
    return np.asarray(x).astype(np.float64)


def striped(idx):
    return np.tile(idx.reshape(-1, 16).T, (8, 1)).astype(np.uint16)


def unstriped(offs):
    return offs[:16].T.reshape(-1).astype(np.int64)


def pack_weight(w):
    k, n = w.shape
    w = f64(np.asarray(w, np.float32).astype(ml_dtypes.bfloat16)).reshape(k // 32, 32, n)
    amax = np.abs(w).max(1)
    byte = np.clip(np.where(amax > 0, np.frexp(amax)[1] - 1 + 127 - 7, 1), 1, 254)
    scaled = (w * np.exp2(127.0 - byte)[:, None, :]).reshape(k, n).astype(np.float32)
    words = np.ascontiguousarray(scaled.reshape(k // 512, 128, 4, n).transpose(0, 1, 3, 2)).astype(ml_dtypes.float8_e4m3fn).view(np.uint8)
    return words, np.ascontiguousarray(byte.astype(np.uint8).reshape(k // 512, 16, n))


def unpack_weight(words, scales):
    g, p, n, _ = words.shape
    vals = np.ascontiguousarray(words).view(ml_dtypes.float8_e4m3fn).astype(np.float64) * np.repeat(np.exp2(scales.astype(np.float64) - 127.0), 8, axis=1)[..., None]
    return vals.transpose(0, 1, 3, 2).reshape(g * 512, n)


def planes(y):
    n, m = y.shape
    v = y.astype(np.float32).astype(ml_dtypes.bfloat16).astype(np.float64).reshape(n // 32, 32, m)
    top = np.abs(v).max(1)
    byte = np.clip(np.where(top > 0, np.frexp(top)[1] - 1 + 127 - 7, 1), 1, 254)
    codes = (v * np.exp2(127.0 - byte)[:, None, :]).reshape(n, m).astype(np.float32).astype(ml_dtypes.float8_e4m3fn).view(np.uint8)
    words = codes.reshape(n // 512, 128, 4, m).transpose(0, 1, 3, 2)
    return np.ascontiguousarray(words), np.ascontiguousarray(byte.astype(np.uint8).reshape(n // 512, 16, m))


def relu(v):
    return np.maximum(v, 0.0)


K, T, S, V, H, N = 512, 1024, 512, 256, 512, 512


def setup_inputs():
    n = np.random.standard_normal
    s = mx_kscale(K)[:, None]
    u = mx_kscale(H)
    near = np.random.permutation(S)
    packed_xT = pack_weight(n((K, T)) * s)
    packed_w1 = pack_weight(n((K, N)) / np.sqrt(K) / s)
    packed_w2 = pack_weight(n((K, N)) / np.sqrt(K) / s)
    packed_w4 = pack_weight(n((H, N)) / np.sqrt(H) / u[:, None])
    return {
        "x_words": packed_xT[0],
        "x_scales": packed_xT[1],
        "w1_words": packed_w1[0],
        "w1_scales": packed_w1[1],
        "w2_words": packed_w2[0],
        "w2_scales": packed_w2[1],
        "w3": (n((K, H)) / np.sqrt(K) / s * u).astype(np.float32),
        "w4_words": packed_w4[0],
        "w4_scales": packed_w4[1],
        "offs": striped(np.random.permutation(T)[:S]),
        "tgt": striped(np.random.permutation(T)[:V]),
        "pos1": striped(near[:V]),
        "pos2": striped(near[V:]),
    }


def reference(x_words, x_scales, w1_words, w1_scales, w2_words, w2_scales, w3, w4_words, w4_scales, offs, tgt, pos1, pos2):
    xq = unpack_weight(x_words, x_scales)[:, unstriped(offs)]
    e = unpack_weight(w2_words, w2_scales).T @ xq
    x_tgt = unpack_weight(x_words, x_scales)[:, unstriped(tgt)]
    y = unpack_weight(w1_words, w1_scales).T @ x_tgt
    a0 = relu(e[:, unstriped(pos1)] * y)
    h = mxq(f64(w3), 0, "e4m3").T @ xq
    a1 = relu(e[:, unstriped(pos2)] * y)
    z = a0 * h[:, unstriped(pos1)] + a1 * h[:, unstriped(pos2)]
    out_0 = unpack_weight(w4_words, w4_scales).T @ mxq(z, 0, "e4m3")
    return (out_0,) + planes(out_0)

@@ -1,0 +1,214 @@
+from contextlib import ExitStack
+
+import concourse.mybir as mybir
+
+K, T, S, V, H, N = 512, 1024, 512, 256, 512, 512
+FLOPS = 2 * K * (S * N + S * H + V * N) + 2 * H * N * V
+
+F32 = mybir.dt.float32
+BF16 = mybir.dt.bfloat16
+I32 = mybir.dt.int32
+U32 = mybir.dt.uint32
+U16 = mybir.dt.uint16
+U8 = mybir.dt.uint8
+FP8X4 = mybir.dt.float8_e4m3fn_x4
+ALU = mybir.AluOpType
+ACT = mybir.ActivationFunctionType
+
+P = 128
+PACK = 4
+HALF = V // 2
+
+
+def words_of(dram):
+    return dram[0].rearrange("p n t -> p (n t)").bitcast(I32)
+
+
+def load_scale_rows(queues, tile, first, step, scales):
+    rows = scales[0].bitcast(I32).rearrange("(q r) c -> r q c", r=4)
+    width = rows.shape[2]
+    for r in range(4):
+        queues[r].dma_start(
+            out=tile[first + r : P : step, :].bitcast(I32),
+            in_=rows[r].unsqueeze(1).to_broadcast([4, 32 // step, width]),
+        )
+
+
+def tile_picked_zdin_relu_po_kernel(
+    tc, x_words, x_scales, w1_words, w1_scales, w2_words, w2_scales, w3, w4_words, w4_scales,
+    offs, tgt, pos1, pos2, out_0, out_1, out_2,
+):
+    nc = tc.nc
+    with ExitStack() as ctx:
+        keep = ctx.enter_context(tc.tile_pool(name="keep", bufs=1))
+        wide = ctx.enter_context(tc.psum_pool(name="wide", bufs=6))
+        narrow = ctx.enter_context(tc.psum_pool(name="narrow", bufs=2))
+
+        def tile(name, shape, dtype):
+            return keep.tile(shape, dtype, name=name, align_bytes=64)
+
+        offs_sb = tile("offs_sb", [P, S // 16], U16)
+        tgt_sb = tile("tgt_sb", [P, V // 16], U16)
+        pos_sb = [tile("pos1_sb", [P, V // 16], U16), tile("pos2_sb", [P, V // 16], U16)]
+        x_w = tile("x_w", [P, T], U32)
+        x_s = tile("x_s", [P, T], U8)
+        w1_w = tile("w1_w", [P, N], U32)
+        w2_w = tile("w2_w", [P, N], U32)
+        w4_w = tile("w4_w", [P, N], U32)
+        w21_s = tile("w21_s", [P, N], U8)
+        w4_s = tile("w4_s", [P, N], U8)
+        w3_raw = tile("w3_raw", [P, PACK, H], F32)
+
+        nc.sync.dma_start(offs_sb[:], offs)
+        load_scale_rows([nc.sync, nc.scalar, nc.sync, nc.scalar], x_s, 0, 4, x_scales)
+        nc.sync.dma_start(out=x_w[:].bitcast(I32), in_=words_of(x_words))
+        nc.sync.dma_start(tgt_sb[:], tgt)
+        nc.sync.dma_start(out=w3_raw[:], in_=w3.rearrange("(p j) c -> p j c", j=PACK))
+        nc.sync.dma_start(out=w2_w[:].bitcast(I32), in_=words_of(w2_words))
+        nc.sync.dma_start(out=w1_w[:].bitcast(I32), in_=words_of(w1_words))
+        nc.sync.dma_start(pos_sb[0][:], pos1)
+        nc.sync.dma_start(pos_sb[1][:], pos2)
+        load_scale_rows([nc.sync, nc.sync, nc.sync, nc.gpsimd], w21_s, 0, 8, w2_scales)
+        load_scale_rows([nc.gpsimd] * 4, w21_s, 4, 8, w1_scales)
+        nc.sync.dma_start(out=w4_w[:].bitcast(I32), in_=words_of(w4_words))
+        load_scale_rows([nc.sync] * 4, w4_s, 0, 4, w4_scales)
+
+        def deal(copy, name, src, dtype):
+            dst = tile(name, [P, N], dtype)
+            if dtype == U8:
+                copy(out=dst[:].rearrange("p (t m) -> p t m", t=PACK), in_=src[:].rearrange("p (m t) -> p t m", t=PACK))
+            else:
+                copy(out=dst[:].rearrange("p (t m) -> p m t", t=PACK), in_=src[:].rearrange("p (m t) -> p m t", t=PACK))
+            return dst
+
+        xq_w = tile("xq_w", [P, S], U32)
+        xq_s = tile("xq_s", [P, S], U8)
+        xt_w = tile("xt_w", [P, V], U32)
+        xt_s = tile("xt_s", [P, V], U8)
+        w3_bf = tile("w3_bf", [P, PACK, P, PACK], BF16)
+
+        def w3_views(first, last):
+            return dict(
+                out=w3_bf[:, :, first:last, :].rearrange("p t m j -> p m j t"),
+                in_=w3_raw[:, :, PACK * first : PACK * last].rearrange("p j (m t) -> p m j t", t=PACK),
+            )
+
+        nc.vector.tensor_copy(out=xq_s[:], in_=x_s[:].indirect(offs_sb[:]))
+        nc.vector.tensor_copy(out=xq_w[:], in_=x_w[:].indirect(offs_sb[:]))
+        nc.vector.tensor_copy(out=xt_s[:], in_=x_s[:].indirect(tgt_sb[:]))
+        nc.vector.tensor_copy(out=xt_w[:], in_=x_w[:].indirect(tgt_sb[:]))
+        nc.scalar.activation(func=ACT.Copy, **w3_views(0, 48))
+        nc.vector.tensor_copy(**w3_views(48, P))
+        w3_dw = tile("w3_dw", [P, H], U32)
+        w3_ds = tile("w3_ds", [P, H], U8)
+        nc.vector.quantize_mx(
+            out=w3_dw[:].bitcast(FP8X4), scales=w3_ds[:], in_=w3_bf[:].rearrange("p t m j -> p (t m j)")
+        )
+
+        w2_dw = deal(nc.scalar.copy, "w2_dw", w2_w, U32)
+        w1_dw = deal(nc.scalar.copy, "w1_dw", w1_w, U32)
+        w21_ds = deal(nc.vector.tensor_copy, "w21_ds", w21_s, U8)
+
+        def product(out, w_words, w_scales, first, t, x_codes, x_bytes):
+            cols = slice(t * P, (t + 1) * P)
+            nc.tensor.matmul_mx(
+                out=out, lhsT=w_words[:, cols].bitcast(FP8X4), lhsT_scale=w_scales[first:P, cols],
+                rhs=x_codes.bitcast(FP8X4), rhs_scale=x_bytes, start=True, stop=True,
+            )
+
+        e_sb = [tile("e_sb%d" % t, [P, S], F32) for t in range(PACK)]
+        h_sb = [tile("h_sb%d" % t, [P, S], F32) for t in range(PACK)]
+        y_sb = [tile("y_sb%d" % u, [P, 2, V], F32) for u in range(2)]
+        ey = [tile("ey%d" % t, [P, 2, V], F32) for t in range(PACK)]
+        hg = [tile("hg%d" % t, [P, 2, V], F32) for t in range(PACK)]
+        terms = tile("terms", [P, PACK, 2, V], F32)
+
+        def make_e(t, copy):
+            bank = wide.tile([P, S], F32, name="bank")
+            product(bank[:], w2_dw, w21_ds, 0, t, xq_w[:], xq_s[:])
+            copy(out=e_sb[t][:], in_=bank[:])
+
+        def make_y(u, copy):
+            pair = narrow.tile([P, 2, V], F32, name="pair")
+            for i in range(2):
+                product(pair[:, i, :], w1_dw, w21_ds, 4, 2 * u + i, xt_w[:], xt_s[:])
+            copy(out=y_sb[u][:], in_=pair[:])
+
+        def make_h(t):
+            bank = wide.tile([P, S], F32, name="bank")
+            product(bank[:], w3_dw, w3_ds, 0, t, xq_w[:], xq_s[:])
+            nc.scalar.copy(out=h_sb[t][:], in_=bank[:])
+
+        def offsets(d, vs):
+            return pos_sb[d][:, vs.start // 16 : vs.stop // 16]
+
+        def fetch_e(t, vs):
+            for d in range(2):
+                nc.vector.tensor_tensor(
+                    out=ey[t][:, d, vs], in0=e_sb[t][:].indirect(offsets(d, vs)), in1=y_sb[t // 2][:, t % 2, vs], op=ALU.mult
+                )
+
+        def fetch_h(t, vs):
+            for d in range(2):
+                nc.scalar.activation(out=hg[t][:, d, vs], in_=h_sb[t][:].indirect(offsets(d, vs)), func=ACT.Copy)
+
+        def weigh(t, vs):
+            nc.vector.scalar_tensor_tensor(
+                out=terms[:, t, :, vs], in0=ey[t][:, :, vs], scalar=0.0, in1=hg[t][:, :, vs], op0=ALU.max, op1=ALU.mult
+            )
+
+        whole = slice(0, V)
+        halves = [slice(0, HALF), slice(HALF, V)]
+        make_h(0)
+        make_e(0, nc.vector.tensor_copy)
+        make_y(0, nc.vector.tensor_copy)
+        for t in range(PACK - 1):
+            fetch_h(t, whole)
+            fetch_e(t, whole)
+            make_e(t + 1, nc.scalar.copy)
+            if t == 1:
+                make_y(1, nc.scalar.copy)
+            make_h(t + 1)
+            weigh(t, whole)
+        for vs in halves:
+            fetch_h(3, vs)
+            fetch_e(3, vs)
+        w4_ds = deal(nc.vector.tensor_copy, "w4_ds", w4_s, U8)
+        w4_dw = deal(nc.scalar.copy, "w4_dw", w4_w, U32)
+
+        o_w = tile("o_w", [P, V], U32)
+        o_s = tile("o_s", [P, V], U8)
+        out_rows = out_0.rearrange("(p t) v -> p t v", t=PACK)
+        z_q = []
+        for a, vs in enumerate(halves):
+            weigh(3, vs)
+        for a, vs in enumerate(halves):
+            z_bf = tile("z_bf%d" % a, [P, HALF * PACK], BF16)
+            nc.vector.tensor_tensor(
+                out=z_bf[:].rearrange("p (c i t) -> p c t i", i=4, t=PACK),
+                in0=terms[:, :, 0, vs].rearrange("p t (c i) -> p c t i", i=4),
+                in1=terms[:, :, 1, vs].rearrange("p t (c i) -> p c t i", i=4),
+                op=ALU.add,
+            )
+            z_w = tile("z_w%d" % a, [P, HALF], U32)
+            z_s = tile("z_s%d" % a, [P, HALF], U8)
+            nc.vector.quantize_mx(out=z_w[:].bitcast(FP8X4), scales=z_s[:], in_=z_bf[:])
+            z_q.append((z_w, z_s))
+        for a, vs in enumerate(halves):
+            bank = wide.tile([P, PACK, HALF], F32, name="bank")
+            for t in range(PACK):
+                product(bank[:, t, :], w4_dw, w4_ds, 0, t, z_q[a][0][:], z_q[a][1][:])
+            o_sb = tile("o_sb%d" % a, [P, PACK, HALF], F32)
+            nc.scalar.copy(out=o_sb[:], in_=bank[:])
+            nc.sync.dma_start(out=out_rows[:, :, vs], in_=o_sb[:])
+            o_bf = tile("o_bf%d" % a, [P, HALF * PACK], BF16)
+            nc.vector.tensor_copy(
+                out=o_bf[:].rearrange("p (c i t) -> p c t i", i=4, t=PACK),
+                in_=o_sb[:].rearrange("p t (c i) -> p c t i", i=4),
+            )
+            nc.vector.quantize_mx(out=o_w[:, vs].bitcast(FP8X4), scales=o_s[:, vs], in_=o_bf[:])
+        nc.sync.dma_start(out=words_of(out_1), in_=o_w[:].bitcast(I32))
+        scale_rows = out_2[0].bitcast(I32)
+        for q in range(4):
+            queue = nc.scalar if q % 2 == 0 else nc.sync
+            queue.dma_start(out=scale_rows[4 * q : 4 * q + 4, :], in_=o_s[32 * q : 32 * q + 4, :].bitcast(I32))

@@ -24,14 +24,10 @@ def words_of(dram):
     return dram[0].rearrange("p n t -> p (n t)").bitcast(I32)
 
 
-def load_scale_rows(queues, tile, first, step, scales):
-    rows = scales[0].bitcast(I32).rearrange("(q r) c -> r q c", r=4)
-    width = rows.shape[2]
-    for r in range(4):
-        queues[r].dma_start(
-            out=tile[first + r : P : step, :].bitcast(I32),
-            in_=rows[r].unsqueeze(1).to_broadcast([4, 32 // step, width]),
-        )
+def load_scale_rows(queue, tile, first, scales, quadrants):
+    rows = scales[0].bitcast(I32)
+    for q in quadrants:
+        queue.dma_start(out=tile[32 * q + first : 32 * q + first + 4, :].bitcast(I32), in_=rows[4 * q : 4 * q + 4, :])
 
 
 def tile_picked_zdin_relu_po_kernel(
@@ -44,8 +40,8 @@ def tile_picked_zdin_relu_po_kernel(
         wide = ctx.enter_context(tc.psum_pool(name="wide", bufs=6))
         narrow = ctx.enter_context(tc.psum_pool(name="narrow", bufs=2))
 
-        def tile(name, shape, dtype):
-            return keep.tile(shape, dtype, name=name, align_bytes=64)
+        def tile(name, shape, dtype, tag=None):
+            return keep.tile(shape, dtype, name=name, tag=tag or name, align_bytes=64)
 
         offs_sb = tile("offs_sb", [P, S // 16], U16)
         tgt_sb = tile("tgt_sb", [P, V // 16], U16)
@@ -55,26 +51,37 @@ def tile_picked_zdin_relu_po_kernel(
         w1_w = tile("w1_w", [P, N], U32)
         w2_w = tile("w2_w", [P, N], U32)
         w4_w = tile("w4_w", [P, N], U32)
-        w21_s = tile("w21_s", [P, N], U8)
+        w_s = tile("w_s", [P, N], U8)
         w4_s = tile("w4_s", [P, N], U8)
-        w3_raw = tile("w3_raw", [P, PACK, H], F32)
+        w3_raw = [tile("w3_raw%d" % a, [P, PACK, H // 2], F32) for a in range(2)]
+        w3_rows = w3.rearrange("(p j) c -> p j c", j=PACK)
 
+        nc.gpsimd.memset(w_s[:].bitcast(I32), 0)
+        nc.vector.memset(w4_s[:].bitcast(I32), 0)
         nc.sync.dma_start(offs_sb[:], offs)
-        load_scale_rows([nc.sync, nc.scalar, nc.sync, nc.scalar], x_s, 0, 4, x_scales)
-        nc.sync.dma_start(out=x_w[:].bitcast(I32), in_=words_of(x_words))
         nc.sync.dma_start(tgt_sb[:], tgt)
-        nc.sync.dma_start(out=w3_raw[:], in_=w3.rearrange("(p j) c -> p j c", j=PACK))
+        x_rows = x_scales[0].bitcast(I32)
+        for q in range(4):
+            queue = nc.scalar if q < 2 else nc.sync
+            queue.dma_start(
+                out=x_s[32 * q : 32 * q + 32, :].bitcast(I32),
+                in_=x_rows[4 * q : 4 * q + 4, :].unsqueeze(0).to_broadcast([8, 4, T // 4]),
+            )
+        nc.sync.dma_start(out=x_w[:].bitcast(I32), in_=words_of(x_words))
+        nc.sync.dma_start(out=w3_raw[0][:], in_=w3_rows[:, :, 0 : H // 2])
+        load_scale_rows(nc.gpsimd, w_s, 4, w1_scales, range(1, 4))
+        load_scale_rows(nc.sync, w_s, 0, w2_scales, range(4))
+        load_scale_rows(nc.sync, w_s, 4, w1_scales, range(1))
+        nc.sync.dma_start(out=w3_raw[1][:], in_=w3_rows[:, :, H // 2 : H])
         nc.sync.dma_start(out=w2_w[:].bitcast(I32), in_=words_of(w2_words))
         nc.sync.dma_start(out=w1_w[:].bitcast(I32), in_=words_of(w1_words))
         nc.sync.dma_start(pos_sb[0][:], pos1)
         nc.sync.dma_start(pos_sb[1][:], pos2)
-        load_scale_rows([nc.sync, nc.sync, nc.sync, nc.gpsimd], w21_s, 0, 8, w2_scales)
-        load_scale_rows([nc.gpsimd] * 4, w21_s, 4, 8, w1_scales)
         nc.sync.dma_start(out=w4_w[:].bitcast(I32), in_=words_of(w4_words))
-        load_scale_rows([nc.sync] * 4, w4_s, 0, 4, w4_scales)
+        load_scale_rows(nc.sync, w4_s, 0, w4_scales, range(4))
 
-        def deal(copy, name, src, dtype):
-            dst = tile(name, [P, N], dtype)
+        def deal(copy, name, src, dtype, tag=None):
+            dst = tile(name, [P, N], dtype, tag)
             if dtype == U8:
                 copy(out=dst[:].rearrange("p (t m) -> p t m", t=PACK), in_=src[:].rearrange("p (m t) -> p t m", t=PACK))
             else:
@@ -87,27 +94,29 @@ def tile_picked_zdin_relu_po_kernel(
         xt_s = tile("xt_s", [P, V], U8)
         w3_bf = tile("w3_bf", [P, PACK, P, PACK], BF16)
 
-        def w3_views(first, last):
+        def w3_views(a, first, last):
             return dict(
-                out=w3_bf[:, :, first:last, :].rearrange("p t m j -> p m j t"),
-                in_=w3_raw[:, :, PACK * first : PACK * last].rearrange("p j (m t) -> p m j t", t=PACK),
+                out=w3_bf[:, :, 64 * a + first : 64 * a + last, :].rearrange("p t m j -> p m j t"),
+                in_=w3_raw[a][:, :, PACK * first : PACK * last].rearrange("p j (m t) -> p m j t", t=PACK),
             )
 
         nc.vector.tensor_copy(out=xq_s[:], in_=x_s[:].indirect(offs_sb[:]))
         nc.vector.tensor_copy(out=xq_w[:], in_=x_w[:].indirect(offs_sb[:]))
         nc.vector.tensor_copy(out=xt_s[:], in_=x_s[:].indirect(tgt_sb[:]))
         nc.vector.tensor_copy(out=xt_w[:], in_=x_w[:].indirect(tgt_sb[:]))
-        nc.scalar.activation(func=ACT.Copy, **w3_views(0, 48))
-        nc.vector.tensor_copy(**w3_views(48, P))
+        nc.scalar.activation(func=ACT.Copy, **w3_views(0, 0, 64))
+        nc.scalar.activation(func=ACT.Copy, **w3_views(1, 0, 20))
+        nc.vector.tensor_copy(**w3_views(1, 20, 64))
         w3_dw = tile("w3_dw", [P, H], U32)
         w3_ds = tile("w3_ds", [P, H], U8)
         nc.vector.quantize_mx(
             out=w3_dw[:].bitcast(FP8X4), scales=w3_ds[:], in_=w3_bf[:].rearrange("p t m j -> p (t m j)")
         )
-
         w2_dw = deal(nc.scalar.copy, "w2_dw", w2_w, U32)
         w1_dw = deal(nc.scalar.copy, "w1_dw", w1_w, U32)
-        w21_ds = deal(nc.vector.tensor_copy, "w21_ds", w21_s, U8)
+        w_ds = deal(nc.vector.tensor_copy, "w_ds", w_s, U8, "w3_raw1")
+        w4_dw = deal(nc.vector.tensor_copy, "w4_dw", w4_w, U32, "w3_bf")
+        w4_ds = deal(nc.vector.tensor_copy, "w4_ds", w4_s, U8, "w_s")
 
         def product(out, w_words, w_scales, first, t, x_codes, x_bytes):
             cols = slice(t * P, (t + 1) * P)
@@ -125,13 +134,13 @@ def tile_picked_zdin_relu_po_kernel(
 
         def make_e(t, copy):
             bank = wide.tile([P, S], F32, name="bank")
-            product(bank[:], w2_dw, w21_ds, 0, t, xq_w[:], xq_s[:])
+            product(bank[:], w2_dw, w_ds, 0, t, xq_w[:], xq_s[:])
             copy(out=e_sb[t][:], in_=bank[:])
 
         def make_y(u, copy):
             pair = narrow.tile([P, 2, V], F32, name="pair")
             for i in range(2):
-                product(pair[:, i, :], w1_dw, w21_ds, 4, 2 * u + i, xt_w[:], xt_s[:])
+                product(pair[:, i, :], w1_dw, w_ds, 4, 2 * u + i, xt_w[:], xt_s[:])
             copy(out=y_sb[u][:], in_=pair[:])
 
         def make_h(t):
@@ -160,21 +169,19 @@ def tile_picked_zdin_relu_po_kernel(
         whole = slice(0, V)
         halves = [slice(0, HALF), slice(HALF, V)]
         make_h(0)
-        make_e(0, nc.vector.tensor_copy)
+        make_e(0, nc.scalar.copy)
         make_y(0, nc.vector.tensor_copy)
         for t in range(PACK - 1):
-            fetch_h(t, whole)
             fetch_e(t, whole)
+            fetch_h(t, whole)
             make_e(t + 1, nc.scalar.copy)
-            if t == 1:
-                make_y(1, nc.scalar.copy)
             make_h(t + 1)
             weigh(t, whole)
+            if t == 0:
+                make_y(1, nc.vector.tensor_copy)
+        fetch_e(PACK - 1, whole)
         for vs in halves:
-            fetch_h(3, vs)
-            fetch_e(3, vs)
-        w4_ds = deal(nc.vector.tensor_copy, "w4_ds", w4_s, U8)
-        w4_dw = deal(nc.scalar.copy, "w4_dw", w4_w, U32)
+            fetch_h(PACK - 1, vs)
 
         o_w = tile("o_w", [P, V], U32)
         o_s = tile("o_s", [P, V], U8)
@@ -199,13 +206,13 @@ def tile_picked_zdin_relu_po_kernel(
             for t in range(PACK):
                 product(bank[:, t, :], w4_dw, w4_ds, 0, t, z_q[a][0][:], z_q[a][1][:])
             o_sb = tile("o_sb%d" % a, [P, PACK, HALF], F32)
+            o_bf = tile("o_bf%d" % a, [P, HALF * PACK], BF16)
+            if a == 0:
+                nc.scalar.copy(out=o_bf[:].rearrange("p (v t) -> p v t", t=PACK), in_=bank[:].rearrange("p t v -> p v t"))
+            else:
+                nc.vector.tensor_copy(out=o_bf[:].rearrange("p (v t) -> p v t", t=PACK), in_=bank[:].rearrange("p t v -> p v t"))
             nc.scalar.copy(out=o_sb[:], in_=bank[:])
             nc.sync.dma_start(out=out_rows[:, :, vs], in_=o_sb[:])
-            o_bf = tile("o_bf%d" % a, [P, HALF * PACK], BF16)
-            nc.vector.tensor_copy(
-                out=o_bf[:].rearrange("p (c i t) -> p c t i", i=4, t=PACK),
-                in_=o_sb[:].rearrange("p t (c i) -> p c t i", i=4),
-            )
             nc.vector.quantize_mx(out=o_w[:, vs].bitcast(FP8X4), scales=o_s[:, vs], in_=o_bf[:])
         nc.sync.dma_start(out=words_of(out_1), in_=o_w[:].bitcast(I32))
         scale_rows = out_2[0].bitcast(I32)

from contextlib import ExitStack

import concourse.mybir as mybir

K, T, S, V, H, N = 512, 1024, 512, 256, 512, 512
FLOPS = 2 * K * (S * N + S * H + V * N) + 2 * H * N * V

F32 = mybir.dt.float32
BF16 = mybir.dt.bfloat16
I32 = mybir.dt.int32
U32 = mybir.dt.uint32
U16 = mybir.dt.uint16
U8 = mybir.dt.uint8
FP8X4 = mybir.dt.float8_e4m3fn_x4
ALU = mybir.AluOpType
ACT = mybir.ActivationFunctionType

P = 128
PACK = 4
HALF = V // 2


def words_of(dram):
    return dram[0].rearrange("p n t -> p (n t)").bitcast(I32)


def load_scale_rows(queue, tile, first, scales, quadrants):
    rows = scales[0].bitcast(I32)
    for q in quadrants:
        queue.dma_start(out=tile[32 * q + first : 32 * q + first + 4, :].bitcast(I32), in_=rows[4 * q : 4 * q + 4, :])


def tile_picked_zdin_relu_po_kernel(
    tc, x_words, x_scales, w1_words, w1_scales, w2_words, w2_scales, w3, w4_words, w4_scales,
    offs, tgt, pos1, pos2, out_0, out_1, out_2,
):
    nc = tc.nc
    with ExitStack() as ctx:
        keep = ctx.enter_context(tc.tile_pool(name="keep", bufs=1))
        wide = ctx.enter_context(tc.psum_pool(name="wide", bufs=6))
        narrow = ctx.enter_context(tc.psum_pool(name="narrow", bufs=2))

        def tile(name, shape, dtype, tag=None):
            return keep.tile(shape, dtype, name=name, tag=tag or name, align_bytes=64)

        offs_sb = tile("offs_sb", [P, S // 16], U16)
        tgt_sb = tile("tgt_sb", [P, V // 16], U16)
        pos_sb = [tile("pos1_sb", [P, V // 16], U16), tile("pos2_sb", [P, V // 16], U16)]
        x_w = tile("x_w", [P, T], U32)
        x_s = tile("x_s", [P, T], U8)
        w1_w = tile("w1_w", [P, N], U32)
        w2_w = tile("w2_w", [P, N], U32)
        w4_w = tile("w4_w", [P, N], U32)
        w_s = tile("w_s", [P, N], U8)
        w4_s = tile("w4_s", [P, N], U8)
        w3_raw = [tile("w3_raw%d" % a, [P, PACK, H // 2], F32) for a in range(2)]
        w3_rows = w3.rearrange("(p j) c -> p j c", j=PACK)

        nc.gpsimd.memset(w_s[:].bitcast(I32), 0)
        nc.vector.memset(w4_s[:].bitcast(I32), 0)
        nc.sync.dma_start(offs_sb[:], offs)
        nc.sync.dma_start(tgt_sb[:], tgt)
        x_rows = x_scales[0].bitcast(I32)
        for q in range(4):
            queue = nc.scalar if q < 2 else nc.sync
            queue.dma_start(
                out=x_s[32 * q : 32 * q + 32, :].bitcast(I32),
                in_=x_rows[4 * q : 4 * q + 4, :].unsqueeze(0).to_broadcast([8, 4, T // 4]),
            )
        nc.sync.dma_start(out=x_w[:].bitcast(I32), in_=words_of(x_words))
        nc.sync.dma_start(out=w3_raw[0][:], in_=w3_rows[:, :, 0 : H // 2])
        load_scale_rows(nc.gpsimd, w_s, 4, w1_scales, range(1, 4))
        load_scale_rows(nc.sync, w_s, 0, w2_scales, range(4))
        load_scale_rows(nc.sync, w_s, 4, w1_scales, range(1))
        nc.sync.dma_start(out=w3_raw[1][:], in_=w3_rows[:, :, H // 2 : H])
        nc.sync.dma_start(out=w2_w[:].bitcast(I32), in_=words_of(w2_words))
        nc.sync.dma_start(out=w1_w[:].bitcast(I32), in_=words_of(w1_words))
        nc.sync.dma_start(pos_sb[0][:], pos1)
        nc.sync.dma_start(pos_sb[1][:], pos2)
        nc.sync.dma_start(out=w4_w[:].bitcast(I32), in_=words_of(w4_words))
        load_scale_rows(nc.sync, w4_s, 0, w4_scales, range(4))

        def deal(copy, name, src, dtype, tag=None):
            dst = tile(name, [P, N], dtype, tag)
            if dtype == U8:
                copy(out=dst[:].rearrange("p (t m) -> p t m", t=PACK), in_=src[:].rearrange("p (m t) -> p t m", t=PACK))
            else:
                copy(out=dst[:].rearrange("p (t m) -> p m t", t=PACK), in_=src[:].rearrange("p (m t) -> p m t", t=PACK))
            return dst

        xq_w = tile("xq_w", [P, S], U32)
        xq_s = tile("xq_s", [P, S], U8)
        xt_w = tile("xt_w", [P, V], U32)
        xt_s = tile("xt_s", [P, V], U8)
        w3_bf = tile("w3_bf", [P, PACK, P, PACK], BF16)

        def w3_views(a, first, last):
            return dict(
                out=w3_bf[:, :, 64 * a + first : 64 * a + last, :].rearrange("p t m j -> p m j t"),
                in_=w3_raw[a][:, :, PACK * first : PACK * last].rearrange("p j (m t) -> p m j t", t=PACK),
            )

        nc.vector.tensor_copy(out=xq_s[:], in_=x_s[:].indirect(offs_sb[:]))
        nc.vector.tensor_copy(out=xq_w[:], in_=x_w[:].indirect(offs_sb[:]))
        nc.vector.tensor_copy(out=xt_s[:], in_=x_s[:].indirect(tgt_sb[:]))
        nc.vector.tensor_copy(out=xt_w[:], in_=x_w[:].indirect(tgt_sb[:]))
        nc.scalar.activation(func=ACT.Copy, **w3_views(0, 0, 64))
        nc.scalar.activation(func=ACT.Copy, **w3_views(1, 0, 20))
        nc.vector.tensor_copy(**w3_views(1, 20, 64))
        w3_dw = tile("w3_dw", [P, H], U32)
        w3_ds = tile("w3_ds", [P, H], U8)
        nc.vector.quantize_mx(
            out=w3_dw[:].bitcast(FP8X4), scales=w3_ds[:], in_=w3_bf[:].rearrange("p t m j -> p (t m j)")
        )
        w2_dw = deal(nc.scalar.copy, "w2_dw", w2_w, U32)
        w1_dw = deal(nc.scalar.copy, "w1_dw", w1_w, U32)
        w_ds = deal(nc.vector.tensor_copy, "w_ds", w_s, U8, "w3_raw1")
        w4_dw = deal(nc.vector.tensor_copy, "w4_dw", w4_w, U32, "w3_bf")
        w4_ds = deal(nc.vector.tensor_copy, "w4_ds", w4_s, U8, "w_s")

        def product(out, w_words, w_scales, first, t, x_codes, x_bytes):
            cols = slice(t * P, (t + 1) * P)
            nc.tensor.matmul_mx(
                out=out, lhsT=w_words[:, cols].bitcast(FP8X4), lhsT_scale=w_scales[first:P, cols],
                rhs=x_codes.bitcast(FP8X4), rhs_scale=x_bytes, start=True, stop=True,
            )

        e_sb = [tile("e_sb%d" % t, [P, S], F32) for t in range(PACK)]
        h_sb = [tile("h_sb%d" % t, [P, S], F32) for t in range(PACK)]
        y_sb = [tile("y_sb%d" % u, [P, 2, V], F32) for u in range(2)]
        ey = [tile("ey%d" % t, [P, 2, V], F32) for t in range(PACK)]
        hg = [tile("hg%d" % t, [P, 2, V], F32) for t in range(PACK)]
        terms = tile("terms", [P, PACK, 2, V], F32)

        def make_e(t, copy):
            bank = wide.tile([P, S], F32, name="bank")
            product(bank[:], w2_dw, w_ds, 0, t, xq_w[:], xq_s[:])
            copy(out=e_sb[t][:], in_=bank[:])

        def make_y(u, copy):
            pair = narrow.tile([P, 2, V], F32, name="pair")
            for i in range(2):
                product(pair[:, i, :], w1_dw, w_ds, 4, 2 * u + i, xt_w[:], xt_s[:])
            copy(out=y_sb[u][:], in_=pair[:])

        def make_h(t):
            bank = wide.tile([P, S], F32, name="bank")
            product(bank[:], w3_dw, w3_ds, 0, t, xq_w[:], xq_s[:])
            nc.scalar.copy(out=h_sb[t][:], in_=bank[:])

        def offsets(d, vs):
            return pos_sb[d][:, vs.start // 16 : vs.stop // 16]

        def fetch_e(t, vs):
            for d in range(2):
                nc.vector.tensor_tensor(
                    out=ey[t][:, d, vs], in0=e_sb[t][:].indirect(offsets(d, vs)), in1=y_sb[t // 2][:, t % 2, vs], op=ALU.mult
                )

        def fetch_h(t, vs):
            for d in range(2):
                nc.scalar.activation(out=hg[t][:, d, vs], in_=h_sb[t][:].indirect(offsets(d, vs)), func=ACT.Copy)

        def weigh(t, vs):
            nc.vector.scalar_tensor_tensor(
                out=terms[:, t, :, vs], in0=ey[t][:, :, vs], scalar=0.0, in1=hg[t][:, :, vs], op0=ALU.max, op1=ALU.mult
            )

        whole = slice(0, V)
        halves = [slice(0, HALF), slice(HALF, V)]
        make_h(0)
        make_e(0, nc.scalar.copy)
        make_y(0, nc.vector.tensor_copy)
        for t in range(PACK - 1):
            fetch_e(t, whole)
            fetch_h(t, whole)
            make_e(t + 1, nc.scalar.copy)
            make_h(t + 1)
            weigh(t, whole)
            if t == 0:
                make_y(1, nc.vector.tensor_copy)
        fetch_e(PACK - 1, whole)
        for vs in halves:
            fetch_h(PACK - 1, vs)

        o_w = tile("o_w", [P, V], U32)
        o_s = tile("o_s", [P, V], U8)
        out_rows = out_0.rearrange("(p t) v -> p t v", t=PACK)
        z_q = []
        for a, vs in enumerate(halves):
            weigh(3, vs)
        for a, vs in enumerate(halves):
            z_bf = tile("z_bf%d" % a, [P, HALF * PACK], BF16)
            nc.vector.tensor_tensor(
                out=z_bf[:].rearrange("p (c i t) -> p c t i", i=4, t=PACK),
                in0=terms[:, :, 0, vs].rearrange("p t (c i) -> p c t i", i=4),
                in1=terms[:, :, 1, vs].rearrange("p t (c i) -> p c t i", i=4),
                op=ALU.add,
            )
            z_w = tile("z_w%d" % a, [P, HALF], U32)
            z_s = tile("z_s%d" % a, [P, HALF], U8)
            nc.vector.quantize_mx(out=z_w[:].bitcast(FP8X4), scales=z_s[:], in_=z_bf[:])
            z_q.append((z_w, z_s))
        for a, vs in enumerate(halves):
            bank = wide.tile([P, PACK, HALF], F32, name="bank")
            for t in range(PACK):
                product(bank[:, t, :], w4_dw, w4_ds, 0, t, z_q[a][0][:], z_q[a][1][:])
            o_sb = tile("o_sb%d" % a, [P, PACK, HALF], F32)
            o_bf = tile("o_bf%d" % a, [P, HALF * PACK], BF16)
            if a == 0:
                nc.scalar.copy(out=o_bf[:].rearrange("p (v t) -> p v t", t=PACK), in_=bank[:].rearrange("p t v -> p v t"))
            else:
                nc.vector.tensor_copy(out=o_bf[:].rearrange("p (v t) -> p v t", t=PACK), in_=bank[:].rearrange("p t v -> p v t"))
            nc.scalar.copy(out=o_sb[:], in_=bank[:])
            nc.sync.dma_start(out=out_rows[:, :, vs], in_=o_sb[:])
            nc.vector.quantize_mx(out=o_w[:, vs].bitcast(FP8X4), scales=o_s[:, vs], in_=o_bf[:])
        nc.sync.dma_start(out=words_of(out_1), in_=o_w[:].bitcast(I32))
        scale_rows = out_2[0].bitcast(I32)
        for q in range(4):
            queue = nc.scalar if q % 2 == 0 else nc.sync
            queue.dma_start(out=scale_rows[4 * q : 4 * q + 4, :], in_=o_s[32 * q : 32 * q + 4, :].bitcast(I32))
